import numpy as np
CORES = [2,10,130,138]
N = 4
ROUNDS = 4
def setup_inputs(rng):
    return {"x": rng.standard_normal((N, ROUNDS, 128, 256), dtype=np.float32)}
def reference(x):
    s = x.sum(axis=0, dtype=np.float64).astype(x.dtype)
    return {"y": np.broadcast_to(s, (N,) + s.shape)}

@@ -1,0 +1,137 @@
+from concourse.bass import RemoteDMATransfer, DstId
+from concourse.mybir import AluOpType
+
+NW = 1
+R = 128 // NW
+HR = R // 2
+
+SCRATCH = {
+    "img": ("dram", [8 * NW, 128, R], "float32"),
+}
+LOCAL = ["stA", "stB", "acA", "acB", "yL", "yS", "yO", "yT"]
+REMOTE = ["a1a", "a1b", "a2", "a3", "f3", "cr", "a4"]
+SEMAPHORES = ["sent"] + [n + str(w) for w in range(4) for n in LOCAL + REMOTE]
+
+M_ROUND = (0, 3)
+S_ROUND = (1, 2)
+LO, HI = 0x0F, 0xF0
+
+
+def rank_program(g, core, T, topo):
+    rank = T.rank_of(core)
+    if rank is None:
+        return
+    p, h = rank & 1, rank >> 1
+    J, O = h ^ p, 1 - (h ^ p)
+    mate, peer = T.cores[rank ^ 1], T.cores[rank ^ 2]
+    m_own, m_oth = M_ROUND[p], M_ROUND[1 - p]
+    s_own, s_oth = S_ROUND[h], S_ROUND[1 - h]
+    img, x, y = T.img, T.x, T.y
+
+    def did(dst):
+        rid, pid = topo.addr(dst, core)
+        return DstId(rid=rid, pnc=pid)
+
+    to_m, to_w = did(mate), did(peer)
+
+    def pair(a, b, base=0):
+        lo, hi = min(a, b), max(a, b)
+        return slice(base + lo, base + hi + 1, hi - lo)
+
+    own, oth = pair(m_own, s_own), pair(m_oth, s_oth)
+
+    q = T.sem
+    table = {
+        "stA": (q.stA0, q.stA1, q.stA2, q.stA3),
+        "stB": (q.stB0, q.stB1, q.stB2, q.stB3),
+        "acA": (q.acA0, q.acA1, q.acA2, q.acA3),
+        "acB": (q.acB0, q.acB1, q.acB2, q.acB3),
+        "yL": (q.yL0, q.yL1, q.yL2, q.yL3),
+        "yS": (q.yS0, q.yS1, q.yS2, q.yS3),
+        "yO": (q.yO0, q.yO1, q.yO2, q.yO3),
+        "yT": (q.yT0, q.yT1, q.yT2, q.yT3),
+        "a1a": (q.a1a0, q.a1a1, q.a1a2, q.a1a3),
+        "a1b": (q.a1b0, q.a1b1, q.a1b2, q.a1b3),
+        "a2": (q.a20, q.a21, q.a22, q.a23),
+        "a3": (q.a30, q.a31, q.a32, q.a33),
+        "f3": (q.f30, q.f31, q.f32, q.f33),
+        "cr": (q.cr0, q.cr1, q.cr2, q.cr3),
+        "a4": (q.a40, q.a41, q.a42, q.a43),
+    }
+
+    def S(name, w):
+        return table[name][w]
+
+    def u(w, j, k):
+        return img[(2 * w + j) * 4 + k]
+
+    def us(w, j, a, b):
+        return img[pair(a, b, (2 * w + j) * 4)]
+
+    def rows(w, j):
+        return slice(w * R + j * HR, w * R + j * HR + HR)
+
+    def copy2(name, w, src_m, dst_m, src_w, dst_w):
+        g.remote_dma_fused(
+            [RemoteDMATransfer(dst_ids=[to_m], dma_engine_mask=LO, remote_sem=S(name, w), src=src_m, dst=dst_m),
+             RemoteDMATransfer(dst_ids=[to_w], dma_engine_mask=HI, remote_sem=S(name, w), src=src_w, dst=dst_w)],
+            local_sem=q.sent)
+
+    W = range(NW)
+    sent = 0
+    for w in W:
+        g.dma_start(us(w, J, m_oth, s_oth), x[oth, rows(w, J), :]).then_inc(S("stA", w), 16)
+        g.dma_start(us(w, O, m_oth, s_oth), x[oth, rows(w, O), :]).then_inc(S("stB", w), 16)
+    for w in W:
+        g.wait_ge(S("stA", w), 16)
+        copy2("a1a", w, u(w, J, m_oth), u(w, J, m_oth), u(w, J, s_oth), u(w, J, s_oth))
+        g.wait_ge(S("stB", w), 16)
+        copy2("a1b", w, u(w, O, m_oth), u(w, O, m_oth), u(w, O, s_oth), u(w, O, s_oth))
+        sent += 16
+    for w in W:
+        g.wait_ge(S("a1a", w), 8)
+        g.dma_start(us(w, O, m_own, s_own), x[own, rows(w, O), :], accum_op=AluOpType.add,
+                    max_dma_last_dim=8192).then_inc(S("acA", w), 16)
+        g.wait_ge(S("acA", w), 16)
+        copy2("a2", w, u(w, O, s_own), u(w, O, m_own), u(w, O, m_own), u(w, O, s_own))
+        sent += 8
+    for w in W:
+        g.wait_ge(S("a1b", w), 8)
+        g.dma_start(us(w, J, m_own, s_own), x[own, rows(w, J), :], accum_op=AluOpType.add,
+                    max_dma_last_dim=8192).then_inc(S("acB", w), 16)
+    for w in W:
+        g.wait_ge(S("acB", w), 16)
+        g.dma_start(y[own, rows(w, J), :], us(w, J, m_own, s_own)).then_inc(S("yL", w), 16)
+    for w in W:
+        g.wait_ge(S("a2", w), 8)
+        g.remote_dma_fused(
+            [RemoteDMATransfer(dst_ids=[to_w, to_m], dma_engine_mask=LO, remote_sem=S("a3", w), alu_op=1,
+                               srcs=[u(w, J, m_own), u(w, J, s_oth)], dsts=[u(w, J, m_own), u(w, J, m_own)]),
+             RemoteDMATransfer(dst_ids=[to_m, to_w], dma_engine_mask=HI, remote_sem=S("a3", w), alu_op=1,
+                               srcs=[u(w, J, s_own), u(w, J, m_oth)], dsts=[u(w, J, s_own), u(w, J, s_own)])],
+            local_sem=S("f3", w))
+        g.wait_ge(S("yL", w), 16)
+        g.dma_start(y[own, rows(w, J), :], us(w, J, m_oth, s_oth), accum_op=AluOpType.add,
+                    max_dma_last_dim=8192).then_inc(S("yS", w), 16)
+    for w in W:
+        g.wait_ge(S("yS", w), 16)
+        g.wait_ge(S("f3", w), 8)
+        g.remote_dma_fused(
+            [RemoteDMATransfer(dst_ids=[to_m], dma_engine_mask=0x01, remote_sem=S("cr", w)),
+             RemoteDMATransfer(dst_ids=[to_w], dma_engine_mask=0x02, remote_sem=S("cr", w))],
+            local_sem=q.sent)
+        sent += 2
+    for w in W:
+        g.wait_ge(S("a3", w), 16)
+        g.wait_ge(S("cr", w), 2)
+        copy2("a4", w, u(w, O, m_own), u(w, O, m_own), u(w, O, s_own), u(w, O, s_own))
+        sent += 8
+        b = (2 * w + O) * 4
+        g.dma_start(y[:, rows(w, O), :], img[b:b + 4]).then_inc(S("yO", w), 16)
+    for w in W:
+        g.wait_ge(S("a4", w), 8)
+        g.dma_start(y[oth, rows(w, J), :], us(w, J, m_oth, s_oth)).then_inc(S("yT", w), 16)
+    for w in W:
+        g.wait_ge(S("yO", w), 16)
+        g.wait_ge(S("yT", w), 16)
+    g.wait_ge(q.sent, sent)

@@ -1,20 +1,15 @@
 from concourse.bass import RemoteDMATransfer, DstId
 from concourse.mybir import AluOpType
 
-NW = 1
-R = 128 // NW
-HR = R // 2
-
 SCRATCH = {
-    "img": ("dram", [8 * NW, 128, R], "float32"),
+    "img": ("dram", [8, 128, 128], "float32"),
 }
-LOCAL = ["stA", "stB", "acA", "acB", "yL", "yS", "yO", "yT"]
-REMOTE = ["a1a", "a1b", "a2", "a3", "f3", "cr", "a4"]
-SEMAPHORES = ["sent"] + [n + str(w) for w in range(4) for n in LOCAL + REMOTE]
+SEMAPHORES = ["sent", "stA", "stB", "acA", "acB", "yL", "yS", "yO", "yT", "a1a", "a1b", "a2", "a3", "f3", "cr", "a4"]
 
 M_ROUND = (0, 3)
 S_ROUND = (1, 2)
 LO, HI = 0x0F, 0xF0
+ADD = AluOpType.add
 
 
 def rank_program(g, core, T, topo):
@@ -26,7 +21,7 @@ def rank_program(g, core, T, topo):
     mate, peer = T.cores[rank ^ 1], T.cores[rank ^ 2]
     m_own, m_oth = M_ROUND[p], M_ROUND[1 - p]
     s_own, s_oth = S_ROUND[h], S_ROUND[1 - h]
-    img, x, y = T.img, T.x, T.y
+    img, x, y, q = T.img, T.x, T.y, T.sem
 
     def did(dst):
         rid, pid = topo.addr(dst, core)
@@ -40,98 +35,56 @@ def rank_program(g, core, T, topo):
 
     own, oth = pair(m_own, s_own), pair(m_oth, s_oth)
 
-    q = T.sem
-    table = {
-        "stA": (q.stA0, q.stA1, q.stA2, q.stA3),
-        "stB": (q.stB0, q.stB1, q.stB2, q.stB3),
-        "acA": (q.acA0, q.acA1, q.acA2, q.acA3),
-        "acB": (q.acB0, q.acB1, q.acB2, q.acB3),
-        "yL": (q.yL0, q.yL1, q.yL2, q.yL3),
-        "yS": (q.yS0, q.yS1, q.yS2, q.yS3),
-        "yO": (q.yO0, q.yO1, q.yO2, q.yO3),
-        "yT": (q.yT0, q.yT1, q.yT2, q.yT3),
-        "a1a": (q.a1a0, q.a1a1, q.a1a2, q.a1a3),
-        "a1b": (q.a1b0, q.a1b1, q.a1b2, q.a1b3),
-        "a2": (q.a20, q.a21, q.a22, q.a23),
-        "a3": (q.a30, q.a31, q.a32, q.a33),
-        "f3": (q.f30, q.f31, q.f32, q.f33),
-        "cr": (q.cr0, q.cr1, q.cr2, q.cr3),
-        "a4": (q.a40, q.a41, q.a42, q.a43),
-    }
+    def u(j, k):
+        return img[j * 4 + k]
 
-    def S(name, w):
-        return table[name][w]
+    def us(j, a, b):
+        return img[pair(a, b, j * 4)]
 
-    def u(w, j, k):
-        return img[(2 * w + j) * 4 + k]
+    def rows(j):
+        return slice(j * 64, j * 64 + 64)
 
-    def us(w, j, a, b):
-        return img[pair(a, b, (2 * w + j) * 4)]
-
-    def rows(w, j):
-        return slice(w * R + j * HR, w * R + j * HR + HR)
-
-    def copy2(name, w, src_m, dst_m, src_w, dst_w):
+    def copy2(sem, src_m, dst_m, src_w, dst_w):
         g.remote_dma_fused(
-            [RemoteDMATransfer(dst_ids=[to_m], dma_engine_mask=LO, remote_sem=S(name, w), src=src_m, dst=dst_m),
-             RemoteDMATransfer(dst_ids=[to_w], dma_engine_mask=HI, remote_sem=S(name, w), src=src_w, dst=dst_w)],
+            [RemoteDMATransfer(dst_ids=[to_m], dma_engine_mask=LO, remote_sem=sem, src=src_m, dst=dst_m),
+             RemoteDMATransfer(dst_ids=[to_w], dma_engine_mask=HI, remote_sem=sem, src=src_w, dst=dst_w)],
             local_sem=q.sent)
 
-    W = range(NW)
-    sent = 0
-    for w in W:
-        g.dma_start(us(w, J, m_oth, s_oth), x[oth, rows(w, J), :]).then_inc(S("stA", w), 16)
-        g.dma_start(us(w, O, m_oth, s_oth), x[oth, rows(w, O), :]).then_inc(S("stB", w), 16)
-    for w in W:
-        g.wait_ge(S("stA", w), 16)
-        copy2("a1a", w, u(w, J, m_oth), u(w, J, m_oth), u(w, J, s_oth), u(w, J, s_oth))
-        g.wait_ge(S("stB", w), 16)
-        copy2("a1b", w, u(w, O, m_oth), u(w, O, m_oth), u(w, O, s_oth), u(w, O, s_oth))
-        sent += 16
-    for w in W:
-        g.wait_ge(S("a1a", w), 8)
-        g.dma_start(us(w, O, m_own, s_own), x[own, rows(w, O), :], accum_op=AluOpType.add,
-                    max_dma_last_dim=8192).then_inc(S("acA", w), 16)
-        g.wait_ge(S("acA", w), 16)
-        copy2("a2", w, u(w, O, s_own), u(w, O, m_own), u(w, O, m_own), u(w, O, s_own))
-        sent += 8
-    for w in W:
-        g.wait_ge(S("a1b", w), 8)
-        g.dma_start(us(w, J, m_own, s_own), x[own, rows(w, J), :], accum_op=AluOpType.add,
-                    max_dma_last_dim=8192).then_inc(S("acB", w), 16)
-    for w in W:
-        g.wait_ge(S("acB", w), 16)
-        g.dma_start(y[own, rows(w, J), :], us(w, J, m_own, s_own)).then_inc(S("yL", w), 16)
-    for w in W:
-        g.wait_ge(S("a2", w), 8)
-        g.remote_dma_fused(
-            [RemoteDMATransfer(dst_ids=[to_w, to_m], dma_engine_mask=LO, remote_sem=S("a3", w), alu_op=1,
-                               srcs=[u(w, J, m_own), u(w, J, s_oth)], dsts=[u(w, J, m_own), u(w, J, m_own)]),
-             RemoteDMATransfer(dst_ids=[to_m, to_w], dma_engine_mask=HI, remote_sem=S("a3", w), alu_op=1,
-                               srcs=[u(w, J, s_own), u(w, J, m_oth)], dsts=[u(w, J, s_own), u(w, J, s_own)])],
-            local_sem=S("f3", w))
-        g.wait_ge(S("yL", w), 16)
-        g.dma_start(y[own, rows(w, J), :], us(w, J, m_oth, s_oth), accum_op=AluOpType.add,
-                    max_dma_last_dim=8192).then_inc(S("yS", w), 16)
-    for w in W:
-        g.wait_ge(S("yS", w), 16)
-        g.wait_ge(S("f3", w), 8)
-        g.remote_dma_fused(
-            [RemoteDMATransfer(dst_ids=[to_m], dma_engine_mask=0x01, remote_sem=S("cr", w)),
-             RemoteDMATransfer(dst_ids=[to_w], dma_engine_mask=0x02, remote_sem=S("cr", w))],
-            local_sem=q.sent)
-        sent += 2
-    for w in W:
-        g.wait_ge(S("a3", w), 16)
-        g.wait_ge(S("cr", w), 2)
-        copy2("a4", w, u(w, O, m_own), u(w, O, m_own), u(w, O, s_own), u(w, O, s_own))
-        sent += 8
-        b = (2 * w + O) * 4
-        g.dma_start(y[:, rows(w, O), :], img[b:b + 4]).then_inc(S("yO", w), 16)
-    for w in W:
-        g.wait_ge(S("a4", w), 8)
-        g.dma_start(y[oth, rows(w, J), :], us(w, J, m_oth, s_oth)).then_inc(S("yT", w), 16)
-    for w in W:
-        g.wait_ge(S("yO", w), 16)
-        g.wait_ge(S("yT", w), 16)
-    g.wait_ge(q.sent, sent)
+    g.dma_start(us(J, m_oth, s_oth), x[oth, rows(J), :]).then_inc(q.stA, 16)
+    g.dma_start(us(O, m_oth, s_oth), x[oth, rows(O), :]).then_inc(q.stB, 16)
+    g.wait_ge(q.stA, 16)
+    copy2(q.a1a, u(J, m_oth), u(J, m_oth), u(J, s_oth), u(J, s_oth))
+    g.wait_ge(q.stB, 16)
+    copy2(q.a1b, u(O, m_oth), u(O, m_oth), u(O, s_oth), u(O, s_oth))
+    g.wait_ge(q.a1a, 8)
+    g.dma_start(us(O, m_own, s_own), x[own, rows(O), :], accum_op=ADD, max_dma_last_dim=8192).then_inc(q.acA, 16)
+    g.wait_ge(q.acA, 16)
+    copy2(q.a2, u(O, s_own), u(O, m_own), u(O, m_own), u(O, s_own))
+    g.wait_ge(q.a1b, 8)
+    g.dma_start(us(J, m_own, s_own), x[own, rows(J), :], accum_op=ADD, max_dma_last_dim=8192).then_inc(q.acB, 16)
+    g.wait_ge(q.acB, 16)
+    g.dma_start(y[own, rows(J), :], us(J, m_own, s_own)).then_inc(q.yL, 16)
+    g.wait_ge(q.a2, 8)
+    g.remote_dma_fused(
+        [RemoteDMATransfer(dst_ids=[to_w, to_m], dma_engine_mask=LO, remote_sem=q.a3, alu_op=1,
+                           srcs=[u(J, m_own), u(J, s_oth)], dsts=[u(J, m_own), u(J, m_own)]),
+         RemoteDMATransfer(dst_ids=[to_m, to_w], dma_engine_mask=HI, remote_sem=q.a3, alu_op=1,
+                           srcs=[u(J, s_own), u(J, m_oth)], dsts=[u(J, s_own), u(J, s_own)])],
+        local_sem=q.f3)
+    g.wait_ge(q.yL, 16)
+    g.dma_start(y[own, rows(J), :], us(J, m_oth, s_oth), accum_op=ADD, max_dma_last_dim=8192).then_inc(q.yS, 16)
+    g.wait_ge(q.f3, 8)
+    g.remote_dma_fused(
+        [RemoteDMATransfer(dst_ids=[to_m], dma_engine_mask=0x01, remote_sem=q.cr),
+         RemoteDMATransfer(dst_ids=[to_w], dma_engine_mask=0x02, remote_sem=q.cr)],
+        local_sem=q.sent)
+    g.wait_ge(q.a3, 16)
+    g.wait_ge(q.cr, 2)
+    copy2(q.a4, u(O, m_own), u(O, s_own), u(O, s_own), u(O, m_own))
+    g.dma_start(y[:, rows(O), :], img[O * 4:O * 4 + 4]).then_inc(q.yO, 16)
+    g.wait_ge(q.a4, 8)
+    g.dma_start(y[oth, rows(J), :], us(J, m_own, s_own)).then_inc(q.yT, 16)
+    g.wait_ge(q.yS, 16)
+    g.wait_ge(q.yO, 16)
+    g.wait_ge(q.yT, 16)
+    g.wait_ge(q.sent, 8 + 8 + 8 + 2 + 8)

@@ -58,10 +58,10 @@ def rank_program(g, core, T, topo):
     copy2(q.a1b, u(O, m_oth), u(O, m_oth), u(O, s_oth), u(O, s_oth))
     g.wait_ge(q.a1a, 8)
     g.dma_start(us(O, m_own, s_own), x[own, rows(O), :], accum_op=ADD, max_dma_last_dim=8192).then_inc(q.acA, 16)
-    g.wait_ge(q.acA, 16)
-    copy2(q.a2, u(O, s_own), u(O, m_own), u(O, m_own), u(O, s_own))
     g.wait_ge(q.a1b, 8)
     g.dma_start(us(J, m_own, s_own), x[own, rows(J), :], accum_op=ADD, max_dma_last_dim=8192).then_inc(q.acB, 16)
+    g.wait_ge(q.acA, 16)
+    copy2(q.a2, u(O, s_own), u(O, m_own), u(O, m_own), u(O, s_own))
     g.wait_ge(q.acB, 16)
     g.dma_start(y[own, rows(J), :], us(J, m_own, s_own)).then_inc(q.yL, 16)
     g.wait_ge(q.a2, 8)

from concourse.bass import RemoteDMATransfer, DstId
from concourse.mybir import AluOpType

SCRATCH = {
    "img": ("dram", [8, 128, 128], "float32"),
}
SEMAPHORES = ["sent", "stA", "stB", "acA", "acB", "yL", "yS", "yO", "yT", "a1a", "a1b", "a2", "a3", "f3", "cr", "a4"]

M_ROUND = (0, 3)
S_ROUND = (1, 2)
LO, HI = 0x0F, 0xF0
ADD = AluOpType.add


def rank_program(g, core, T, topo):
    rank = T.rank_of(core)
    if rank is None:
        return
    p, h = rank & 1, rank >> 1
    J, O = h ^ p, 1 - (h ^ p)
    mate, peer = T.cores[rank ^ 1], T.cores[rank ^ 2]
    m_own, m_oth = M_ROUND[p], M_ROUND[1 - p]
    s_own, s_oth = S_ROUND[h], S_ROUND[1 - h]
    img, x, y, q = T.img, T.x, T.y, T.sem

    def did(dst):
        rid, pid = topo.addr(dst, core)
        return DstId(rid=rid, pnc=pid)

    to_m, to_w = did(mate), did(peer)

    def pair(a, b, base=0):
        lo, hi = min(a, b), max(a, b)
        return slice(base + lo, base + hi + 1, hi - lo)

    own, oth = pair(m_own, s_own), pair(m_oth, s_oth)

    def u(j, k):
        return img[j * 4 + k]

    def us(j, a, b):
        return img[pair(a, b, j * 4)]

    def rows(j):
        return slice(j * 64, j * 64 + 64)

    def copy2(sem, src_m, dst_m, src_w, dst_w):
        g.remote_dma_fused(
            [RemoteDMATransfer(dst_ids=[to_m], dma_engine_mask=LO, remote_sem=sem, src=src_m, dst=dst_m),
             RemoteDMATransfer(dst_ids=[to_w], dma_engine_mask=HI, remote_sem=sem, src=src_w, dst=dst_w)],
            local_sem=q.sent)

    g.dma_start(us(J, m_oth, s_oth), x[oth, rows(J), :]).then_inc(q.stA, 16)
    g.dma_start(us(O, m_oth, s_oth), x[oth, rows(O), :]).then_inc(q.stB, 16)
    g.wait_ge(q.stA, 16)
    copy2(q.a1a, u(J, m_oth), u(J, m_oth), u(J, s_oth), u(J, s_oth))
    g.wait_ge(q.stB, 16)
    copy2(q.a1b, u(O, m_oth), u(O, m_oth), u(O, s_oth), u(O, s_oth))
    g.wait_ge(q.a1a, 8)
    g.dma_start(us(O, m_own, s_own), x[own, rows(O), :], accum_op=ADD, max_dma_last_dim=8192).then_inc(q.acA, 16)
    g.wait_ge(q.a1b, 8)
    g.dma_start(us(J, m_own, s_own), x[own, rows(J), :], accum_op=ADD, max_dma_last_dim=8192).then_inc(q.acB, 16)
    g.wait_ge(q.acA, 16)
    copy2(q.a2, u(O, s_own), u(O, m_own), u(O, m_own), u(O, s_own))
    g.wait_ge(q.acB, 16)
    g.dma_start(y[own, rows(J), :], us(J, m_own, s_own)).then_inc(q.yL, 16)
    g.wait_ge(q.a2, 8)
    g.remote_dma_fused(
        [RemoteDMATransfer(dst_ids=[to_w, to_m], dma_engine_mask=LO, remote_sem=q.a3, alu_op=1,
                           srcs=[u(J, m_own), u(J, s_oth)], dsts=[u(J, m_own), u(J, m_own)]),
         RemoteDMATransfer(dst_ids=[to_m, to_w], dma_engine_mask=HI, remote_sem=q.a3, alu_op=1,
                           srcs=[u(J, s_own), u(J, m_oth)], dsts=[u(J, s_own), u(J, s_own)])],
        local_sem=q.f3)
    g.wait_ge(q.yL, 16)
    g.dma_start(y[own, rows(J), :], us(J, m_oth, s_oth), accum_op=ADD, max_dma_last_dim=8192).then_inc(q.yS, 16)
    g.wait_ge(q.f3, 8)
    g.remote_dma_fused(
        [RemoteDMATransfer(dst_ids=[to_m], dma_engine_mask=0x01, remote_sem=q.cr),
         RemoteDMATransfer(dst_ids=[to_w], dma_engine_mask=0x02, remote_sem=q.cr)],
        local_sem=q.sent)
    g.wait_ge(q.a3, 16)
    g.wait_ge(q.cr, 2)
    copy2(q.a4, u(O, m_own), u(O, s_own), u(O, s_own), u(O, m_own))
    g.dma_start(y[:, rows(O), :], img[O * 4:O * 4 + 4]).then_inc(q.yO, 16)
    g.wait_ge(q.a4, 8)
    g.dma_start(y[oth, rows(J), :], us(J, m_own, s_own)).then_inc(q.yT, 16)
    g.wait_ge(q.yS, 16)
    g.wait_ge(q.yO, 16)
    g.wait_ge(q.yT, 16)
    g.wait_ge(q.sent, 8 + 8 + 8 + 2 + 8)
